import numpy as np, ml_dtypes
CORES = [7,39,87,119,135,167,215,247,263,295,343,375,391,423,471,503]
N = 16
KT, C = 4, 64
B = 2
def setup_inputs(rng):
    return {"x": rng.standard_normal((N, 128, KT * C), dtype=np.float32).astype(ml_dtypes.bfloat16)}
def setup_inputs_big(rng):
    d = setup_inputs(rng)
    for k in ("x",): d[k] = (d[k].astype(np.float32) * 1024.0).astype(d[k].dtype)
    return d
def setup_inputs_small(rng):
    d = setup_inputs(rng)
    for k in ("x",): d[k] = (d[k].astype(np.float32) * (1 / 1024.0)).astype(d[k].dtype)
    return d
def setup_inputs_apart(rng):
    d = setup_inputs(rng)
    f = (10.0 ** rng.permutation(np.linspace(-1.5, 1.5, N))).astype(np.float32).reshape(N, 1, 1)
    for k in ("x",): d[k] = (d[k].astype(np.float32) * f).astype(d[k].dtype)
    return d
def reference(x):
    X = x.astype(np.float64)
    y = np.full((N, C, (2 * B + 1) * C), np.nan)
    for r in range(N):
        for i in range(2 * B + 1):
            s = (r + i - B) % N
            if s != r: y[r][:, C * i:C * i + C] = sum(X[r][:, C * t:C * t + C].T @ X[s][:, C * t:C * t + C] for t in range(KT))
    return {"y": y.astype(ml_dtypes.bfloat16 if x.dtype != np.float64 else np.float64)}

@@ -1,0 +1,82 @@
+from concourse.bass import DstId, RemoteDMATransfer
+
+C, KT = 64, 4
+
+SCRATCH = {
+    "xs": ("sbuf", [128, KT * C], "bfloat16"),
+    "inA": ("sbuf", [128, KT * C], "bfloat16"),
+    "inB": ("sbuf", [128, KT * C], "bfloat16"),
+    "back": ("sbuf", [128, C], "bfloat16"),
+    "own": ("sbuf", [128, 2 * C], "bfloat16"),
+    "retA": ("sbuf", [128, C], "bfloat16"),
+    "retB": ("sbuf", [128, C], "bfloat16"),
+    "psBack": ("psum", [128, 512], "float32"),
+    "psOwn": ("psum", [128, 512], "float32"),
+}
+SEMAPHORES = ["ld", "arrA", "arrB", "mmBack", "mmOwn", "cpBack", "cpOwn", "gotA", "gotB", "sent", "st"]
+
+
+def _split(mask, parts):
+    bits = [1 << b for b in range(mask.bit_length()) if (mask >> b) & 1]
+    n = len(bits) // parts
+    return [sum(bits[i * n:(i + 1) * n]) for i in range(parts)], n
+
+
+def rank_program(g, core, T, topo):
+    r = T.rank_of(core)
+    if r is None:
+        return
+    n = len(T.cores)
+    S = T.sem
+    nxt, prv2 = T.cores[(r + 1) % n], T.cores[(r - 2) % n]
+    prv, nxt2 = T.cores[(r - 1) % n], T.cores[(r + 2) % n]
+
+    def tile(buf, t):
+        return buf[:, C * t:C * t + C]
+
+    def send(pairs):
+        common = topo.mask(core, pairs[0][0])
+        for d in pairs:
+            common &= topo.mask(core, d[0])
+        masks, per = _split(common, len(pairs))
+        trs = []
+        for (d, src, dst, sem), m in zip(pairs, masks):
+            rid, pid = topo.addr(d, core)
+            trs.append(RemoteDMATransfer(dst_ids=[DstId(rid=rid, pnc=pid)], dma_engine_mask=m, remote_sem=sem,
+                                         src=src, dst=dst))
+        g.remote_dma_fused(trs, local_sem=S.sent)
+        return per
+
+    g.sync.dma_start(T.xs[:], T.x[:]).then_inc(S.ld, 16)
+
+    g.wait_ge(S.ld, 16)
+    per = send([(nxt, T.xs[:], T.inA[:], S.arrA), (prv2, T.xs[:], T.inB[:], S.arrB)])
+
+    my_rack = topo.rack(topo.host(core))
+    srcs = [(prv, T.inA, S.arrA, 0), (nxt2, T.inB, S.arrB, 1)]
+    srcs.sort(key=lambda e: topo.rack(topo.host(e[0])) != my_rack)
+    g.tensor.wait_ge(S.ld, 16)
+    for _, buf, sem, k in srcs:
+        g.tensor.wait_ge(sem, per)
+        for t in range(KT):
+            g.tensor.matmul(T.psBack[C * k:C * k + C, 0:C], tile(buf, t), tile(T.xs, t), t == 0, t == KT - 1).then_inc(S.mmBack, 1)
+        for t in range(KT):
+            g.tensor.matmul(T.psOwn[0:C, C * k:C * k + C], tile(T.xs, t), tile(buf, t), t == 0, t == KT - 1).then_inc(S.mmOwn, 1)
+
+    g.vector.wait_ge(S.mmBack, 2 * KT)
+    g.vector.tensor_copy(T.back[:], T.psBack[:, 0:C]).then_inc(S.cpBack, 1)
+    g.vector.wait_ge(S.mmOwn, 2 * KT)
+    g.vector.tensor_copy(T.own[0:C, :], T.psOwn[0:C, 0:2 * C]).then_inc(S.cpOwn, 1)
+    g.wait_ge(S.cpBack, 1)
+    per2 = send([(prv, T.back[:], T.retA[:], S.gotA), (nxt2, T.back[:], T.retB[:], S.gotB)])
+
+    g.scalar.wait_ge(S.cpOwn, 1)
+    g.scalar.dma_start(T.y[:, 1 * C:2 * C], T.own[0:C, 0:C]).then_inc(S.st, 16)
+    g.scalar.dma_start(T.y[:, 4 * C:5 * C], T.own[0:C, C:2 * C]).then_inc(S.st, 16)
+    g.sync.wait_ge(S.gotA, per2)
+    g.sync.dma_start(T.y[:, 3 * C:4 * C], T.retA[0:C, :]).then_inc(S.st, 16)
+    g.scalar.wait_ge(S.gotB, per2)
+    g.scalar.dma_start(T.y[:, 0:C], T.retB[C:2 * C, :]).then_inc(S.st, 16)
+
+    g.wait_ge(S.sent, 2 * per + 2 * per2)
+    g.wait_ge(S.st, 64)

@@ -4,79 +4,150 @@ C, KT = 64, 4
 
 SCRATCH = {
     "xs": ("sbuf", [128, KT * C], "bfloat16"),
-    "inA": ("sbuf", [128, KT * C], "bfloat16"),
-    "inB": ("sbuf", [128, KT * C], "bfloat16"),
-    "back": ("sbuf", [128, C], "bfloat16"),
+    "in0": ("sbuf", [128, KT * C], "bfloat16"),
+    "in1": ("sbuf", [128, KT * C], "bfloat16"),
+    "back0": ("sbuf", [128, C], "bfloat16"),
+    "back1": ("sbuf", [128, C], "bfloat16"),
     "own": ("sbuf", [128, 2 * C], "bfloat16"),
-    "retA": ("sbuf", [128, C], "bfloat16"),
-    "retB": ("sbuf", [128, C], "bfloat16"),
+    "ret0": ("sbuf", [128, C], "bfloat16"),
+    "ret1": ("sbuf", [128, C], "bfloat16"),
     "psBack": ("psum", [128, 512], "float32"),
     "psOwn": ("psum", [128, 512], "float32"),
 }
-SEMAPHORES = ["ld", "arrA", "arrB", "mmBack", "mmOwn", "cpBack", "cpOwn", "gotA", "gotB", "sent", "st"]
+SEMAPHORES = ["ld", "arr0", "arr1", "mmBack", "mmOwn", "fill", "cpBack", "cpOwn", "got0", "got1", "sent", "st"]
+
+PLAN = {
+    0: ((-2, 2), ((2, (0,)),)),
+    1: ((-2, -1), ((-1, (0, -2)),)),
+    2: ((1, 2), ((2, (0, 1)),)),
+    3: ((-2, -1), ((-2, (0, -1)), (-1, (-2,)))),
+    4: ((1, 2), ((2, (0, 1)), (1, (2,)))),
+    5: ((-2, -1), ((-2, (0, -1)),)),
+    6: ((2, 1), ((1, (0, 2)),)),
+    7: ((2, -2), ((-2, (0,)),)),
+}
 
 
-def _split(mask, parts):
-    bits = [1 << b for b in range(mask.bit_length()) if (mask >> b) & 1]
-    n = len(bits) // parts
-    return [sum(bits[i * n:(i + 1) * n]) for i in range(parts)], n
+def _plan(cores, topo):
+    n = len(cores)
+    rk = [topo.rack(topo.host(c)) for c in cores]
+    holds, rets = [], []
+    for r in range(n):
+        p = 0
+        while p < n and rk[(r - p - 1) % n] == rk[r]:
+            p += 1
+        h, b = PLAN[p]
+        holds.append([(r + o) % n for o in h])
+        rets.append([((r + d) % n, [(r + o) % n for o in ss]) for d, ss in b])
+    return holds, rets
+
+
+def _shares(topo, src, dsts):
+    common = topo.mask(src, dsts[0])
+    for d in dsts:
+        common &= topo.mask(src, d)
+    bits = [1 << b for b in range(common.bit_length()) if (common >> b) & 1]
+    k = len(bits) // len(dsts)
+    return [sum(bits[i * k:(i + 1) * k]) for i in range(len(dsts))], k
 
 
 def rank_program(g, core, T, topo):
     r = T.rank_of(core)
     if r is None:
         return
-    n = len(T.cores)
+    cores = T.cores
+    n = len(cores)
     S = T.sem
-    nxt, prv2 = T.cores[(r + 1) % n], T.cores[(r - 2) % n]
-    prv, nxt2 = T.cores[(r - 1) % n], T.cores[(r + 2) % n]
+    holds, rets = _plan(cores, topo)
+
+    def far(a, b):
+        return topo.rack(topo.host(cores[a])) != topo.rack(topo.host(cores[b]))
+
+    def takers(s):
+        return sorted([d for d in range(n) if s in holds[d]], key=lambda d: not far(s, d))
 
     def tile(buf, t):
         return buf[:, C * t:C * t + C]
 
-    def send(pairs):
-        common = topo.mask(core, pairs[0][0])
-        for d in pairs:
-            common &= topo.mask(core, d[0])
-        masks, per = _split(common, len(pairs))
+    def send(items):
+        masks, k = _shares(topo, core, [cores[d] for d, _, _, _ in items])
         trs = []
-        for (d, src, dst, sem), m in zip(pairs, masks):
-            rid, pid = topo.addr(d, core)
+        for (d, src, dst, sem), m in zip(items, masks):
+            rid, pid = topo.addr(cores[d], core)
             trs.append(RemoteDMATransfer(dst_ids=[DstId(rid=rid, pnc=pid)], dma_engine_mask=m, remote_sem=sem,
                                          src=src, dst=dst))
         g.remote_dma_fused(trs, local_sem=S.sent)
-        return per
+        return k * len(items)
+
+    mine, owed = holds[r], rets[r]
+    buf = {r: T.xs, mine[0]: T.in0, mine[1]: T.in1}
+    left = 0
 
     g.sync.dma_start(T.xs[:], T.x[:]).then_inc(S.ld, 16)
+    fills = 0
+    for k, (d, ss) in enumerate(owed):
+        if len(ss) == 1:
+            g.vector.memset(T["back%d" % k][C:2 * C, :], 0.0).then_inc(S.fill, 1)
+            fills += 1
 
     g.wait_ge(S.ld, 16)
-    per = send([(nxt, T.xs[:], T.inA[:], S.arrA), (prv2, T.xs[:], T.inB[:], S.arrB)])
+    left += send([(d, T.xs[:], T["in%d" % holds[d].index(r)][:], S["arr%d" % holds[d].index(r)]) for d in takers(r)])
 
-    my_rack = topo.rack(topo.host(core))
-    srcs = [(prv, T.inA, S.arrA, 0), (nxt2, T.inB, S.arrB, 1)]
-    srcs.sort(key=lambda e: topo.rack(topo.host(e[0])) != my_rack)
+    groups = [(k, h, d, s) for k, (d, ss) in enumerate(owed) for h, s in enumerate(ss)]
+    have, done = {r}, set()
     g.tensor.wait_ge(S.ld, 16)
-    for _, buf, sem, k in srcs:
-        g.tensor.wait_ge(sem, per)
+    for s0 in sorted(mine, key=lambda s: far(s, r)):
+        j = mine.index(s0)
+        g.tensor.wait_ge(S["arr%d" % j], _shares(topo, cores[s0], [cores[d] for d in takers(s0)])[1])
+        have.add(s0)
+        for grp in groups:
+            k, h, d, s = grp
+            if grp in done or d not in have or s not in have:
+                continue
+            done.add(grp)
+            for t in range(KT):
+                g.tensor.matmul(T.psBack[C * h:C * h + C, C * k:C * k + C], tile(buf[d], t), tile(buf[s], t),
+                                t == 0, t == KT - 1).then_inc(S.mmBack, 1)
         for t in range(KT):
-            g.tensor.matmul(T.psBack[C * k:C * k + C, 0:C], tile(buf, t), tile(T.xs, t), t == 0, t == KT - 1).then_inc(S.mmBack, 1)
-        for t in range(KT):
-            g.tensor.matmul(T.psOwn[0:C, C * k:C * k + C], tile(T.xs, t), tile(buf, t), t == 0, t == KT - 1).then_inc(S.mmOwn, 1)
+            g.tensor.matmul(T.psOwn[0:C, C * j:C * j + C], tile(T.xs, t), tile(buf[s0], t),
+                            t == 0, t == KT - 1).then_inc(S.mmOwn, 1)
 
-    g.vector.wait_ge(S.mmBack, 2 * KT)
-    g.vector.tensor_copy(T.back[:], T.psBack[:, 0:C]).then_inc(S.cpBack, 1)
+    g.vector.wait_ge(S.mmBack, KT * len(groups))
+    for k, (d, ss) in enumerate(owed):
+        rows = C * len(ss)
+        g.vector.tensor_copy(T["back%d" % k][0:rows, :], T.psBack[0:rows, C * k:C * k + C]).then_inc(S.cpBack, 1)
     g.vector.wait_ge(S.mmOwn, 2 * KT)
     g.vector.tensor_copy(T.own[0:C, :], T.psOwn[0:C, 0:2 * C]).then_inc(S.cpOwn, 1)
-    g.wait_ge(S.cpBack, 1)
-    per2 = send([(prv, T.back[:], T.retA[:], S.gotA), (nxt2, T.back[:], T.retB[:], S.gotB)])
 
+    def givers(d):
+        return [(c, k, ss) for c in range(n) for k, (dd, ss) in enumerate(rets[c]) if dd == d]
+
+    if fills:
+        g.wait_ge(S.fill, fills)
+    g.wait_ge(S.cpBack, len(owed))
+    items = []
+    for k, (d, ss) in enumerate(owed):
+        q = [(c, kk) for c, kk, _ in givers(d)].index((r, k))
+        items.append((d, T["back%d" % k][:], T["ret%d" % q][:], S["got%d" % q]))
+    left += send(items)
+
+    def block(s):
+        i = (s - r + 2) % n
+        return T.y[:, C * i:C * i + C]
+
+    stores = 0
     g.scalar.wait_ge(S.cpOwn, 1)
-    g.scalar.dma_start(T.y[:, 1 * C:2 * C], T.own[0:C, 0:C]).then_inc(S.st, 16)
-    g.scalar.dma_start(T.y[:, 4 * C:5 * C], T.own[0:C, C:2 * C]).then_inc(S.st, 16)
-    g.sync.wait_ge(S.gotA, per2)
-    g.sync.dma_start(T.y[:, 3 * C:4 * C], T.retA[0:C, :]).then_inc(S.st, 16)
-    g.scalar.wait_ge(S.gotB, per2)
-    g.scalar.dma_start(T.y[:, 0:C], T.retB[C:2 * C, :]).then_inc(S.st, 16)
+    for j, s in enumerate(mine):
+        g.scalar.dma_start(block(s), T.own[0:C, C * j:C * j + C]).then_inc(S.st, 16)
+        stores += 1
+    queues = [g.sync, g.scalar]
+    for q, (c, k, ss) in enumerate(givers(r)):
+        cnt = _shares(topo, cores[c], [cores[d] for d, _ in rets[c]])[1]
+        for h, s in enumerate(ss):
+            qu = queues[stores % 2]
+            qu.wait_ge(S["got%d" % q], cnt)
+            qu.dma_start(block(s), T["ret%d" % q][C * h:C * h + C, :]).then_inc(S.st, 16)
+            stores += 1
 
-    g.wait_ge(S.sent, 2 * per + 2 * per2)
-    g.wait_ge(S.st, 64)
+    g.wait_ge(S.sent, left)
+    g.wait_ge(S.st, 16 * stores)

from concourse.bass import DstId, RemoteDMATransfer

C, KT = 64, 4

SCRATCH = {
    "xs": ("sbuf", [128, KT * C], "bfloat16"),
    "in0": ("sbuf", [128, KT * C], "bfloat16"),
    "in1": ("sbuf", [128, KT * C], "bfloat16"),
    "back0": ("sbuf", [128, C], "bfloat16"),
    "back1": ("sbuf", [128, C], "bfloat16"),
    "own": ("sbuf", [128, 2 * C], "bfloat16"),
    "ret0": ("sbuf", [128, C], "bfloat16"),
    "ret1": ("sbuf", [128, C], "bfloat16"),
    "psBack": ("psum", [128, 512], "float32"),
    "psOwn": ("psum", [128, 512], "float32"),
}
SEMAPHORES = ["ld", "arr0", "arr1", "mmBack", "mmOwn", "fill", "cpBack", "cpOwn", "got0", "got1", "sent", "st"]

PLAN = {
    0: ((-2, 2), ((2, (0,)),)),
    1: ((-2, -1), ((-1, (0, -2)),)),
    2: ((1, 2), ((2, (0, 1)),)),
    3: ((-2, -1), ((-2, (0, -1)), (-1, (-2,)))),
    4: ((1, 2), ((2, (0, 1)), (1, (2,)))),
    5: ((-2, -1), ((-2, (0, -1)),)),
    6: ((2, 1), ((1, (0, 2)),)),
    7: ((2, -2), ((-2, (0,)),)),
}


def _plan(cores, topo):
    n = len(cores)
    rk = [topo.rack(topo.host(c)) for c in cores]
    holds, rets = [], []
    for r in range(n):
        p = 0
        while p < n and rk[(r - p - 1) % n] == rk[r]:
            p += 1
        h, b = PLAN[p]
        holds.append([(r + o) % n for o in h])
        rets.append([((r + d) % n, [(r + o) % n for o in ss]) for d, ss in b])
    return holds, rets


def _shares(topo, src, dsts):
    common = topo.mask(src, dsts[0])
    for d in dsts:
        common &= topo.mask(src, d)
    bits = [1 << b for b in range(common.bit_length()) if (common >> b) & 1]
    k = len(bits) // len(dsts)
    return [sum(bits[i * k:(i + 1) * k]) for i in range(len(dsts))], k


def rank_program(g, core, T, topo):
    r = T.rank_of(core)
    if r is None:
        return
    cores = T.cores
    n = len(cores)
    S = T.sem
    holds, rets = _plan(cores, topo)

    def far(a, b):
        return topo.rack(topo.host(cores[a])) != topo.rack(topo.host(cores[b]))

    def takers(s):
        return sorted([d for d in range(n) if s in holds[d]], key=lambda d: not far(s, d))

    def tile(buf, t):
        return buf[:, C * t:C * t + C]

    def send(items):
        masks, k = _shares(topo, core, [cores[d] for d, _, _, _ in items])
        trs = []
        for (d, src, dst, sem), m in zip(items, masks):
            rid, pid = topo.addr(cores[d], core)
            trs.append(RemoteDMATransfer(dst_ids=[DstId(rid=rid, pnc=pid)], dma_engine_mask=m, remote_sem=sem,
                                         src=src, dst=dst))
        g.remote_dma_fused(trs, local_sem=S.sent)
        return k * len(items)

    mine, owed = holds[r], rets[r]
    buf = {r: T.xs, mine[0]: T.in0, mine[1]: T.in1}
    left = 0

    g.sync.dma_start(T.xs[:], T.x[:]).then_inc(S.ld, 16)
    fills = 0
    for k, (d, ss) in enumerate(owed):
        if len(ss) == 1:
            g.vector.memset(T["back%d" % k][C:2 * C, :], 0.0).then_inc(S.fill, 1)
            fills += 1

    g.wait_ge(S.ld, 16)
    left += send([(d, T.xs[:], T["in%d" % holds[d].index(r)][:], S["arr%d" % holds[d].index(r)]) for d in takers(r)])

    groups = [(k, h, d, s) for k, (d, ss) in enumerate(owed) for h, s in enumerate(ss)]
    have, done = {r}, set()
    g.tensor.wait_ge(S.ld, 16)
    for s0 in sorted(mine, key=lambda s: far(s, r)):
        j = mine.index(s0)
        g.tensor.wait_ge(S["arr%d" % j], _shares(topo, cores[s0], [cores[d] for d in takers(s0)])[1])
        have.add(s0)
        for grp in groups:
            k, h, d, s = grp
            if grp in done or d not in have or s not in have:
                continue
            done.add(grp)
            for t in range(KT):
                g.tensor.matmul(T.psBack[C * h:C * h + C, C * k:C * k + C], tile(buf[d], t), tile(buf[s], t),
                                t == 0, t == KT - 1).then_inc(S.mmBack, 1)
        for t in range(KT):
            g.tensor.matmul(T.psOwn[0:C, C * j:C * j + C], tile(T.xs, t), tile(buf[s0], t),
                            t == 0, t == KT - 1).then_inc(S.mmOwn, 1)

    g.vector.wait_ge(S.mmBack, KT * len(groups))
    for k, (d, ss) in enumerate(owed):
        rows = C * len(ss)
        g.vector.tensor_copy(T["back%d" % k][0:rows, :], T.psBack[0:rows, C * k:C * k + C]).then_inc(S.cpBack, 1)
    g.vector.wait_ge(S.mmOwn, 2 * KT)
    g.vector.tensor_copy(T.own[0:C, :], T.psOwn[0:C, 0:2 * C]).then_inc(S.cpOwn, 1)

    def givers(d):
        return [(c, k, ss) for c in range(n) for k, (dd, ss) in enumerate(rets[c]) if dd == d]

    if fills:
        g.wait_ge(S.fill, fills)
    g.wait_ge(S.cpBack, len(owed))
    items = []
    for k, (d, ss) in enumerate(owed):
        q = [(c, kk) for c, kk, _ in givers(d)].index((r, k))
        items.append((d, T["back%d" % k][:], T["ret%d" % q][:], S["got%d" % q]))
    left += send(items)

    def block(s):
        i = (s - r + 2) % n
        return T.y[:, C * i:C * i + C]

    stores = 0
    g.scalar.wait_ge(S.cpOwn, 1)
    for j, s in enumerate(mine):
        g.scalar.dma_start(block(s), T.own[0:C, C * j:C * j + C]).then_inc(S.st, 16)
        stores += 1
    queues = [g.sync, g.scalar]
    for q, (c, k, ss) in enumerate(givers(r)):
        cnt = _shares(topo, cores[c], [cores[d] for d, _ in rets[c]])[1]
        for h, s in enumerate(ss):
            qu = queues[stores % 2]
            qu.wait_ge(S["got%d" % q], cnt)
            qu.dma_start(block(s), T["ret%d" % q][C * h:C * h + C, :]).then_inc(S.st, 16)
            stores += 1

    g.wait_ge(S.sent, left)
    g.wait_ge(S.st, 16 * stores)
